import numpy as np
import ml_dtypes


def mxq(x, axis, fmt="e4m3"):
    dtype, down = {"e4m3": (ml_dtypes.float8_e4m3fn, 7), "e5m2": (ml_dtypes.float8_e5m2, 14)}[fmt]
    v = np.moveaxis(np.asarray(x, np.float32).astype(ml_dtypes.bfloat16).astype(np.float64), axis, -1)
    blocks = v.reshape(v.shape[:-1] + (-1, 32))
    amax = np.abs(blocks).max(-1, keepdims=True)
    byte = np.maximum(np.where(amax > 0, np.frexp(amax)[1] - 1 + 127, 0) - down, 1)
    scale = np.exp2(byte - 127.0)
    codes = (blocks / scale).astype(np.float32).astype(dtype).astype(np.float64)
    return np.moveaxis((codes * scale).reshape(v.shape), -1, axis)


WIDE = False


def mx_kscale(k):
    if not WIDE:
        return np.ones(k)
    levels = np.array([10, -10, 5, -5, 0])
    if k % 512:
        return np.exp2(np.random.permutation(np.resize(levels, k // 32))).repeat(32)
    a = np.empty((k // 512, 16))
    for p in range(k // 512):
        a[p, :8] = np.random.permutation(np.resize(levels, 8))
        for g in range(8):
            far = levels[np.abs(levels - a[p, g]) >= 10]
            a[p, g + 8] = far[np.random.randint(len(far))]
    return np.exp2(a.ravel()).repeat(32)


def f64(x):
    return np.asarray(x).astype(np.float64)


def striped(idx):
    return np.tile(idx.reshape(-1, 16).T, (8, 1)).astype(np.uint16)


def unstriped(offs):
    return offs[:16].T.reshape(-1).astype(np.int64)


def pack_weight(w):
    k, n = w.shape
    w = f64(np.asarray(w, np.float32).astype(ml_dtypes.bfloat16)).reshape(k // 32, 32, n)
    amax = np.abs(w).max(1)
    byte = np.clip(np.where(amax > 0, np.frexp(amax)[1] - 1 + 127 - 7, 1), 1, 254)
    scaled = (w * np.exp2(127.0 - byte)[:, None, :]).reshape(k, n).astype(np.float32)
    words = np.ascontiguousarray(scaled.reshape(k // 512, 128, 4, n).transpose(0, 1, 3, 2)).astype(ml_dtypes.float8_e4m3fn).view(np.uint8)
    return words, np.ascontiguousarray(byte.astype(np.uint8).reshape(k // 512, 16, n))


def unpack_weight(words, scales):
    g, p, n, _ = words.shape
    vals = np.ascontiguousarray(words).view(ml_dtypes.float8_e4m3fn).astype(np.float64) * np.repeat(np.exp2(scales.astype(np.float64) - 127.0), 8, axis=1)[..., None]
    return vals.transpose(0, 1, 3, 2).reshape(g * 512, n)


K, T, S, D, N, H = 1024, 2048, 512, 4, 256, 512


def setup_inputs():
    n = np.random.standard_normal
    s = mx_kscale(K)[:, None]
    u = mx_kscale(H)
    packed_xT = pack_weight(n((K, T)) * s)
    return {
        "x_words": packed_xT[0],
        "x_scales": packed_xT[1],
        "w1": (n((K, H)) / np.sqrt(K) / s).astype(np.float32),
        "w2": (n((K, H)) / np.sqrt(K) / s).astype(np.float32),
        "unit": (np.random.uniform(0.6, 1.4, (H, 1)) * u[:, None]).astype(np.float32),
        "w3": (n((H, N)) / np.sqrt(H) / u[:, None]).astype(np.float32),
        "offs": striped(np.random.permutation(T)[:S]),
    }


def reference(x_words, x_scales, w1, w2, unit, w3, offs):
    xq = unpack_weight(x_words, x_scales)[:, unstriped(offs)]
    ec = mxq(f64(w1), 0, "e4m3").T @ xq
    eu = mxq(f64(w2), 0, "e4m3").T @ xq
    dlt = ec - eu
    d2 = (dlt) ** 2
    nrm = np.sqrt(d2.reshape(len(d2), -1, D).mean(axis=2) + 0.1)
    dn = dlt / np.repeat(nrm, D, axis=1)
    dc = dn * ec
    cc2 = (ec) ** 2
    proj = (dc.reshape(len(dc), -1, D).sum(axis=2)) / (cc2.reshape(len(cc2), -1, D).sum(axis=2) + 0.3)
    par = np.repeat(proj, D, axis=1) * ec
    gui = ec + 1.5 * (dn - par) + 0.4 * par
    hid = f64(unit) * gui
    return mxq(f64(w3), 0, "e4m3").T @ mxq(hid, 0, "e4m3")

@@ -1,0 +1,290 @@
+from contextlib import ExitStack
+
+import concourse.mybir as mybir
+from concourse.masks import make_identity
+
+K, T, S, D, N, H = 1024, 2048, 512, 4, 256, 512
+FLOPS = 2 * (2 * K * H * S + H * N * S)
+
+F32 = mybir.dt.float32
+BF16 = mybir.dt.bfloat16
+I32 = mybir.dt.int32
+U32 = mybir.dt.uint32
+U16 = mybir.dt.uint16
+U8 = mybir.dt.uint8
+FP8X4 = mybir.dt.float8_e4m3fn_x4
+ALU = mybir.AluOpType
+ACT = mybir.ActivationFunctionType
+
+P = 128
+PACK = 4
+PASSES = K // (P * PACK)
+V = S // D
+CH = 128
+CHUNKS = H // CH
+CAST = "SSSSSVSVSVSVSVSVSV"
+DC = "VVVV"
+ADD = "VVVV"
+DPE = "0000"
+SPLIT = "1112"
+GSPLIT = 1
+
+
+def tile_picked_yapgui_apg_p_kernel(tc, x_words, x_scales, w1, w2, unit, w3, offs, out):
+    nc = tc.nc
+    with ExitStack() as ctx:
+        keep = ctx.enter_context(tc.tile_pool(name="keep", bufs=1))
+        work = ctx.enter_context(tc.tile_pool(name="work", bufs=4))
+        psum = ctx.enter_context(tc.psum_pool(name="psum", bufs=2))
+
+        offsets = keep.tile([P, S // 16], U16, name="offsets")
+        nc.sync.dma_start(offsets[:], offs)
+
+        scale_table = keep.tile([P, T], U8, name="scale_table", align_bytes=64)
+        nc.vector.memset(scale_table[:].bitcast(I32), 0)
+        word_table = [keep.tile([P, T], U32, name="word_table%d" % o, align_bytes=64) for o in range(PASSES)]
+        w3_raw = keep.tile([P, PACK, N], F32, name="w3_raw")
+        unit_sb = keep.tile([P, CHUNKS], F32, name="unit_sb")
+        raw = {}
+
+        def load_words(o):
+            nc.sync.dma_start(word_table[o][:].bitcast(I32), x_words[o].rearrange("p n t -> p (n t)").bitcast(I32))
+
+        def load_scales():
+            for q in range(4):
+                nc.scalar.dma_start(
+                    scale_table[32 * q : 32 * q + 4 * PASSES, :].bitcast(I32),
+                    x_scales[:, 4 * q : 4 * q + 4, :].bitcast(I32),
+                )
+
+        def load_weights(c, s):
+            for o in range(PASSES):
+                raw[c, s, o] = keep.tile([P, PACK, CH], F32, name="raw%d_%d_%d" % (c, s, o))
+                rows = (w1, w2)[s][512 * o : 512 * (o + 1), CH * c : CH * (c + 1)]
+                nc.sync.dma_start(raw[c, s, o][:], rows.rearrange("(p j) n -> p j n", j=PACK))
+
+        def load_unit():
+            with nc.allow_non_contiguous_dma(reason="one value a partition and chunk"):
+                nc.sync.dma_start(unit_sb[:], unit.rearrange("(c p) o -> p (c o)", p=P))
+
+        load_scales()
+        load_words(0)
+        load_words(1)
+        load_weights(0, 0)
+        load_weights(0, 1)
+        load_weights(1, 0)
+        load_weights(1, 1)
+        load_unit()
+        load_weights(2, 0)
+        load_weights(2, 1)
+        load_weights(3, 0)
+        load_weights(3, 1)
+        nc.sync.dma_start(w3_raw[:], w3.rearrange("(p j) n -> p j n", j=PACK))
+
+
+        ident = keep.tile([P, P], F32, name="ident")
+        make_identity(nc, ident[:])
+
+        x_codes = [keep.tile([P, S], U32, name="x_codes%d" % o, align_bytes=64) for o in range(PASSES)]
+        picked_scales = keep.tile([P, S], U8, name="picked_scales", align_bytes=64)
+        x_planes = keep.tile([P, S], U8, name="x_planes", align_bytes=64)
+
+        def gather_words(o):
+            nc.vector.tensor_copy(x_codes[o][:].rearrange("p (d v) -> p v d", d=D), word_table[o][:].indirect(offsets[:]))
+
+        def gather():
+            gather_words(0)
+            nc.vector.tensor_copy(picked_scales[:], scale_table[:].indirect(offsets[:]))
+            nc.vector.tensor_copy(
+                x_planes[:].rearrange("p (d v) -> p d v", d=D), picked_scales[:].rearrange("p (v d) -> p d v", d=D)
+            )
+            gather_words(1)
+
+        def interleave(engine, dst, src, sign):
+            dst_view = dst.rearrange("p (a i) j -> p a j i", i=4)
+            src_view = src.rearrange("p j (a i) -> p a j i", i=4)
+            if engine == "V":
+                nc.vector.tensor_scalar(dst_view, src_view, sign, None, ALU.mult)
+            elif engine == "G":
+                n = dst_view.shape[1] // GSPLIT
+                for g in range(GSPLIT):
+                    nc.gpsimd.tensor_scalar(dst_view[:, g * n : (g + 1) * n], src_view[:, g * n : (g + 1) * n], sign, 0.0, ALU.mult, ALU.add)
+            else:
+                nc.scalar.activation(dst_view, src_view, ACT.Copy, scale=sign)
+
+        def copy_out(engine, dst, src):
+            if engine == "V":
+                nc.vector.tensor_copy(dst, src)
+            else:
+                nc.scalar.copy(dst, src)
+
+        def quantize(codes, planes, grouped):
+            nc.vector.quantize_mx(out=codes.bitcast(FP8X4), scales=planes, in_=grouped)
+
+        w_codes, w_planes = {}, {}
+
+        def prepare_weights(c):
+            for s in range(2):
+                grouped = work.tile([P, PASSES, CH, PACK], BF16, name="grouped%d" % s, align_bytes=64)
+                for o in range(PASSES):
+                    interleave(CAST[4 * c + 2 * s + o], grouped[:, o], raw[c, s, o][:], (1.0, -1.0)[s])
+                w_codes[c, s] = work.tile([P, PASSES * CH], U32, name="w_codes%d" % s, align_bytes=64)
+                w_planes[c, s] = work.tile([P, PASSES * CH], U8, name="w_planes%d" % s, align_bytes=64)
+                quantize(w_codes[c, s][:], w_planes[c, s][:], grouped[:].rearrange("p o n j -> p (o n j)"))
+
+        banks = {}
+
+        def products(c):
+            for s in range(2):
+                banks[c, s] = psum.tile([P, D, CH], F32, name="pred%d" % s, tag="pred%d" % s)
+                terms = [(0, o) for o in range(PASSES)] if (s == 0 or DPE[c] == "1") else []
+                terms = terms + ([(1, o) for o in range(PASSES)] if s == 1 else [])
+                for d in range(D):
+                    for i, (w, o) in enumerate(terms):
+                        nc.tensor.matmul_mx(
+                            out=banks[c, s][:, d, :],
+                            lhsT=x_codes[o][:, V * d : V * (d + 1)].bitcast(FP8X4),
+                            lhsT_scale=x_planes[4 * o : P, V * d : V * (d + 1)],
+                            rhs=w_codes[c, w][:, CH * o : CH * (o + 1)].bitcast(FP8X4),
+                            rhs_scale=w_planes[c, w][:, CH * o : CH * (o + 1)],
+                            start=(i == 0),
+                            stop=(i == len(terms) - 1),
+                        )
+
+        cond, diff, sums = {}, {}, {}
+
+        def parts(c):
+            n = int(SPLIT[c])
+            return [slice(i * (D // n), (i + 1) * (D // n)) for i in range(n)]
+
+        def squares(c):
+            cond[c] = work.tile([P, D, CH], F32, name="cond")
+            diff[c] = work.tile([P, D, CH], F32, name="diff")
+            cc = work.tile([P, D, CH], F32, name="cc")
+            dd = work.tile([P, D, CH], F32, name="dd")
+            dc = work.tile([P, D, CH], F32, name="dc")
+            if DPE[c] == "1":
+                nc.scalar.copy(diff[c][:], banks[c, 1][:])
+                nc.scalar.activation(dd[:], banks[c, 1][:], ACT.Square)
+                nc.scalar.copy(cond[c][:], banks[c, 0][:])
+            else:
+                for ds in parts(c):
+                    nc.scalar.copy(cond[c][:, ds], banks[c, 0][:, ds])
+                for ds in parts(c):
+                    nc.vector.tensor_tensor(diff[c][:, ds], cond[c][:, ds], banks[c, 1][:, ds], ALU.add)
+                for ds in parts(c):
+                    nc.scalar.activation(dd[:, ds], diff[c][:, ds], ACT.Square)
+            nc.scalar.activation(cc[:], banks[c, 0][:], ACT.Square)
+            for ds in parts(c):
+                if DC[c] == "G":
+                    nc.gpsimd.tensor_tensor(dc[:, ds], diff[c][:, ds], cond[c][:, ds], ALU.mult)
+                elif DC[c] == "P":
+                    nc.vector.tensor_tensor(dc[:, ds], diff[c][:, ds], banks[c, 0][:, ds], ALU.mult)
+                else:
+                    nc.vector.tensor_tensor(dc[:, ds], diff[c][:, ds], cond[c][:, ds], ALU.mult)
+            sums[c] = psum.tile([P, 3, V], F32, name="sums", tag="sums")
+            for i, term in enumerate((cc, dd, dc)):
+                for d in range(D):
+                    nc.tensor.matmul(
+                        sums[c][:, i, :], lhsT=term[:, d, :], rhs=ident[:], is_transpose=True, start=(d == 0), stop=(d == D - 1)
+                    )
+
+        hid = keep.tile([P, D, H], BF16, name="hid")
+        spread = {}
+
+        def statistics(c):
+            inv_norm = work.tile([P, V], F32, name="inv_norm")
+            inv_root = work.tile([P, V], F32, name="inv_root")
+            inv_den = work.tile([P, V], F32, name="inv_den")
+            gain = work.tile([P, V], F32, name="gain")
+            num = work.tile([P, V], F32, name="num")
+            shrink = work.tile([P, V], F32, name="shrink")
+            nc.scalar.activation(inv_norm[:], sums[c][:, 1, :], ACT.Abs_reciprocal_sqrt, scale=0.25 / 2.25, bias=0.1 / 2.25)
+            nc.scalar.activation(inv_root[:], sums[c][:, 0, :], ACT.Abs_reciprocal_sqrt, bias=0.3)
+            nc.scalar.activation(gain[:], inv_norm[:], ACT.Copy, scale=unit_sb[:, c : c + 1])
+            nc.scalar.activation(inv_den[:], inv_root[:], ACT.Square)
+            nc.vector.scalar_tensor_tensor(num[:], sums[c][:, 2, :], -1.1 / 1.5, gain[:], ALU.mult, ALU.mult)
+            nc.vector.tensor_tensor(shrink[:], num[:], inv_den[:], ALU.mult)
+            factors = psum.tile([P, 2, CH], F32, name="factors", tag="factors")
+            nc.tensor.transpose(factors[:, 0, :], gain[:], ident[:])
+            for i, term in enumerate((unit_sb[:, c : c + 1].to_broadcast([P, V]), shrink[:])):
+                nc.tensor.matmul(factors[:, 1, :], lhsT=term, rhs=ident[:], is_transpose=True, start=(i == 0), stop=(i == 1))
+            spread[c] = [factors[:, i, :].unsqueeze(1).to_broadcast([P, D, CH]) for i in range(2)]
+
+        def guide(c):
+            along = work.tile([P, D, CH], F32, name="along")
+            across = work.tile([P, D, CH], F32, name="across")
+            for ds in parts(c):
+                nc.vector.tensor_tensor(across[:, ds], diff[c][:, ds], spread[c][0][:, ds], ALU.mult)
+                nc.vector.tensor_tensor(along[:, ds], cond[c][:, ds], spread[c][1][:, ds], ALU.mult)
+            for ds in parts(c):
+                (nc.gpsimd if ADD[c] == "G" else nc.vector).tensor_tensor(
+                    hid[:, ds, CH * c : CH * (c + 1)], along[:, ds], across[:, ds], ALU.add
+                )
+
+        w3_codes = keep.tile([P, N], U32, name="w3_codes", align_bytes=64)
+        w3_planes = keep.tile([P, N], U8, name="w3_planes", align_bytes=64)
+
+        def prepare_w3():
+            grouped = keep.tile([P, N, PACK], BF16, name="w3_grouped", align_bytes=64)
+            for half in range(2):
+                cols = slice(half * (N // 2), (half + 1) * (N // 2))
+                interleave(CAST[16 + half], grouped[:, cols, :], w3_raw[:, :, cols], 1.0)
+            quantize(w3_codes[:], w3_planes[:], grouped[:].rearrange("p n j -> p (n j)"))
+
+        gather()
+        prepare_weights(0)
+        products(0)
+        squares(0)
+        prepare_weights(1)
+        products(1)
+        squares(1)
+        prepare_weights(2)
+        products(2)
+        statistics(0)
+        squares(2)
+        prepare_weights(3)
+        products(3)
+        statistics(1)
+        guide(0)
+        squares(3)
+        statistics(2)
+        guide(1)
+        statistics(3)
+        guide(2)
+        guide(3)
+        prepare_w3()
+
+        result = [psum.tile([P, D, V], F32, name="result%d" % h, tag=("sums", "factors")[h]) for h in range(N // P)]
+        for d in range(D):
+            turned = psum.tile([P, 2, V], F32, name="turned", tag="pred%d" % (d % 2))
+            words = hid[:, d, :].bitcast(F32)
+            for u in range(2):
+                nc.tensor.transpose(turned[:, u, :], words[:, u : H // 2 : 2], ident[:])
+            hid_k = work.tile([P, V, PACK], BF16, name="hid_k", align_bytes=64)
+            copy_out(
+                "SVSV"[d],
+                hid_k[:].rearrange("p v t -> p (v t)").bitcast(F32).rearrange("p (v u) -> p v u", u=2),
+                turned[:].rearrange("p u v -> p v u"),
+            )
+            hid_codes = work.tile([P, V], U32, name="hid_codes", align_bytes=64)
+            hid_planes = work.tile([P, V], U8, name="hid_planes", align_bytes=64)
+            quantize(hid_codes[:], hid_planes[:], hid_k[:].rearrange("p v t -> p (v t)"))
+            for h in range(N // P):
+                nc.tensor.matmul_mx(
+                    out=result[h][:, d, :],
+                    lhsT=w3_codes[:, P * h : P * (h + 1)].bitcast(FP8X4),
+                    lhsT_scale=w3_planes[:, P * h : P * (h + 1)],
+                    rhs=hid_codes[:].bitcast(FP8X4),
+                    rhs_scale=hid_planes[:],
+                    start=True,
+                    stop=True,
+                )
+        for half in range(2):
+            for h in range(N // P):
+                staged = keep.tile([P, V // 2, D], F32, name="staged%d_%d" % (h, half))
+                groups = slice(half * (V // 2), (half + 1) * (V // 2))
+                copy_out("SV"[h], staged[:], result[h][:, :, groups].rearrange("p d v -> p v d"))
+                nc.sync.dma_start(
+                    out[P * h : P * (h + 1), half * (S // 2) : (half + 1) * (S // 2)], staged[:].rearrange("p v d -> p (v d)")
+                )

@@ -19,257 +19,219 @@ ACT = mybir.ActivationFunctionType
 P = 128
 PACK = 4
 PASSES = K // (P * PACK)
-V = S // D
-CH = 128
-CHUNKS = H // CH
-CAST = "SSSSSVSVSVSVSVSVSV"
-DC = "VVVV"
-ADD = "VVVV"
-DPE = "0000"
-SPLIT = "1112"
-GSPLIT = 1
+GROUPS = S // D
+PLANE_ROWS = 4
+LINE = 4
+QUARTER = H // PACK
+COND, UNCOND = 0, 1
+AMPLIFY = 1.5
+WEAKEN = 1.5 - 0.4
 
 
 def tile_picked_yapgui_apg_p_kernel(tc, x_words, x_scales, w1, w2, unit, w3, offs, out):
     nc = tc.nc
     with ExitStack() as ctx:
         keep = ctx.enter_context(tc.tile_pool(name="keep", bufs=1))
-        work = ctx.enter_context(tc.tile_pool(name="work", bufs=4))
+        work = ctx.enter_context(tc.tile_pool(name="work", bufs=PACK))
         psum = ctx.enter_context(tc.psum_pool(name="psum", bufs=2))
 
         offsets = keep.tile([P, S // 16], U16, name="offsets")
         nc.sync.dma_start(offsets[:], offs)
 
         scale_table = keep.tile([P, T], U8, name="scale_table", align_bytes=64)
-        nc.vector.memset(scale_table[:].bitcast(I32), 0)
+        nc.gpsimd.memset(scale_table[:].bitcast(I32), 0)
         word_table = [keep.tile([P, T], U32, name="word_table%d" % o, align_bytes=64) for o in range(PASSES)]
-        w3_raw = keep.tile([P, PACK, N], F32, name="w3_raw")
-        unit_sb = keep.tile([P, CHUNKS], F32, name="unit_sb")
+
+        def load_words(o, first, last):
+            words = x_words[o].rearrange("p n t -> p (n t)").bitcast(I32)
+            nc.sync.dma_start(word_table[o][:, first:last].bitcast(I32), words[:, first:last])
+
         raw = {}
 
-        def load_words(o):
-            nc.sync.dma_start(word_table[o][:].bitcast(I32), x_words[o].rearrange("p n t -> p (n t)").bitcast(I32))
+        def load_weights(side, o, pieces):
+            span = PACK // pieces
+            for first in range(0, PACK, span):
+                tile = keep.tile([P, PACK, QUARTER * span], F32, name="raw%d_%d_%d" % (side, o, first))
+                rows = (w1, w2)[side][P * PACK * o : P * PACK * (o + 1), QUARTER * first : QUARTER * (first + span)]
+                nc.sync.dma_start(tile[:], rows.rearrange("(p j) n -> p j n", j=PACK))
+                for q in range(span):
+                    raw[side, o, first + q] = tile[:, :, QUARTER * q : QUARTER * (q + 1)]
 
-        def load_scales():
-            for q in range(4):
-                nc.scalar.dma_start(
-                    scale_table[32 * q : 32 * q + 4 * PASSES, :].bitcast(I32),
-                    x_scales[:, 4 * q : 4 * q + 4, :].bitcast(I32),
-                )
-
-        def load_weights(c, s):
-            for o in range(PASSES):
-                raw[c, s, o] = keep.tile([P, PACK, CH], F32, name="raw%d_%d_%d" % (c, s, o))
-                rows = (w1, w2)[s][512 * o : 512 * (o + 1), CH * c : CH * (c + 1)]
-                nc.sync.dma_start(raw[c, s, o][:], rows.rearrange("(p j) n -> p j n", j=PACK))
-
-        def load_unit():
-            with nc.allow_non_contiguous_dma(reason="one value a partition and chunk"):
-                nc.sync.dma_start(unit_sb[:], unit.rearrange("(c p) o -> p (c o)", p=P))
-
-        load_scales()
-        load_words(0)
-        load_words(1)
-        load_weights(0, 0)
-        load_weights(0, 1)
-        load_weights(1, 0)
-        load_weights(1, 1)
-        load_unit()
-        load_weights(2, 0)
-        load_weights(2, 1)
-        load_weights(3, 0)
-        load_weights(3, 1)
+        load_words(0, 0, T // 2)
+        for quadrant in range(P // 32):
+            nc.sync.dma_start(
+                scale_table[32 * quadrant : 32 * quadrant + PLANE_ROWS * PASSES, :].bitcast(I32),
+                x_scales[:, PLANE_ROWS * quadrant : PLANE_ROWS * (quadrant + 1), :].bitcast(I32),
+            )
+        load_words(0, T // 2, T)
+        load_words(1, 0, T)
+        load_weights(COND, 0, 1)
+        load_weights(COND, 1, 1)
+        unit_sb = keep.tile([P, PACK], F32, name="unit_sb")
+        nc.sync.dma_start(unit_sb[:], unit.rearrange("(p t) o -> p (t o)", t=PACK))
+        load_weights(UNCOND, 0, 1)
+        load_weights(UNCOND, 1, 2)
+        w3_raw = keep.tile([P, PACK, N], F32, name="w3_raw")
         nc.sync.dma_start(w3_raw[:], w3.rearrange("(p j) n -> p j n", j=PACK))
 
+        warm = keep.tile([P, 2], F32, name="warm")
+        nc.vector.memset(warm[:, 0:1], 1.0)
+        nc.scalar.activation(warm[:, 1:2], warm[:, 0:1], ACT.Abs_reciprocal_sqrt)
 
         ident = keep.tile([P, P], F32, name="ident")
         make_identity(nc, ident[:])
+        one = keep.tile([P, 1], F32, name="one")
+        nc.gpsimd.memset(one[:], 1.0)
 
-        x_codes = [keep.tile([P, S], U32, name="x_codes%d" % o, align_bytes=64) for o in range(PASSES)]
         picked_scales = keep.tile([P, S], U8, name="picked_scales", align_bytes=64)
         x_planes = keep.tile([P, S], U8, name="x_planes", align_bytes=64)
-
-        def gather_words(o):
+        nc.vector.tensor_copy(picked_scales[:], scale_table[:].indirect(offsets[:]))
+        nc.vector.tensor_copy(
+            x_planes[:].rearrange("p (d v) -> p d v", d=D), picked_scales[:].rearrange("p (v d) -> p d v", d=D)
+        )
+        x_codes = [keep.tile([P, S], U32, name="x_codes%d" % o, align_bytes=64) for o in range(PASSES)]
+        for o in range(PASSES):
             nc.vector.tensor_copy(x_codes[o][:].rearrange("p (d v) -> p v d", d=D), word_table[o][:].indirect(offsets[:]))
 
-        def gather():
-            gather_words(0)
-            nc.vector.tensor_copy(picked_scales[:], scale_table[:].indirect(offsets[:]))
-            nc.vector.tensor_copy(
-                x_planes[:].rearrange("p (d v) -> p d v", d=D), picked_scales[:].rearrange("p (v d) -> p d v", d=D)
-            )
-            gather_words(1)
-
-        def interleave(engine, dst, src, sign):
-            dst_view = dst.rearrange("p (a i) j -> p a j i", i=4)
-            src_view = src.rearrange("p j (a i) -> p a j i", i=4)
-            if engine == "V":
-                nc.vector.tensor_scalar(dst_view, src_view, sign, None, ALU.mult)
-            elif engine == "G":
-                n = dst_view.shape[1] // GSPLIT
-                for g in range(GSPLIT):
-                    nc.gpsimd.tensor_scalar(dst_view[:, g * n : (g + 1) * n], src_view[:, g * n : (g + 1) * n], sign, 0.0, ALU.mult, ALU.add)
-            else:
-                nc.scalar.activation(dst_view, src_view, ACT.Copy, scale=sign)
-
-        def copy_out(engine, dst, src):
-            if engine == "V":
+        def copy_on(vector, dst, src):
+            if vector:
                 nc.vector.tensor_copy(dst, src)
             else:
                 nc.scalar.copy(dst, src)
 
-        def quantize(codes, planes, grouped):
-            nc.vector.quantize_mx(out=codes.bitcast(FP8X4), scales=planes, in_=grouped)
+        def quantize(codes, planes, values):
+            nc.vector.quantize_mx(out=codes.bitcast(FP8X4), scales=planes, in_=values)
 
         w_codes, w_planes = {}, {}
 
-        def prepare_weights(c):
-            for s in range(2):
-                grouped = work.tile([P, PASSES, CH, PACK], BF16, name="grouped%d" % s, align_bytes=64)
-                for o in range(PASSES):
-                    interleave(CAST[4 * c + 2 * s + o], grouped[:, o], raw[c, s, o][:], (1.0, -1.0)[s])
-                w_codes[c, s] = work.tile([P, PASSES * CH], U32, name="w_codes%d" % s, align_bytes=64)
-                w_planes[c, s] = work.tile([P, PASSES * CH], U8, name="w_planes%d" % s, align_bytes=64)
-                quantize(w_codes[c, s][:], w_planes[c, s][:], grouped[:].rearrange("p o n j -> p (o n j)"))
-
-        banks = {}
-
-        def products(c):
-            for s in range(2):
-                banks[c, s] = psum.tile([P, D, CH], F32, name="pred%d" % s, tag="pred%d" % s)
-                terms = [(0, o) for o in range(PASSES)] if (s == 0 or DPE[c] == "1") else []
-                terms = terms + ([(1, o) for o in range(PASSES)] if s == 1 else [])
-                for d in range(D):
-                    for i, (w, o) in enumerate(terms):
-                        nc.tensor.matmul_mx(
-                            out=banks[c, s][:, d, :],
-                            lhsT=x_codes[o][:, V * d : V * (d + 1)].bitcast(FP8X4),
-                            lhsT_scale=x_planes[4 * o : P, V * d : V * (d + 1)],
-                            rhs=w_codes[c, w][:, CH * o : CH * (o + 1)].bitcast(FP8X4),
-                            rhs_scale=w_planes[c, w][:, CH * o : CH * (o + 1)],
-                            start=(i == 0),
-                            stop=(i == len(terms) - 1),
-                        )
-
-        cond, diff, sums = {}, {}, {}
-
-        def parts(c):
-            n = int(SPLIT[c])
-            return [slice(i * (D // n), (i + 1) * (D // n)) for i in range(n)]
-
-        def squares(c):
-            cond[c] = work.tile([P, D, CH], F32, name="cond")
-            diff[c] = work.tile([P, D, CH], F32, name="diff")
-            cc = work.tile([P, D, CH], F32, name="cc")
-            dd = work.tile([P, D, CH], F32, name="dd")
-            dc = work.tile([P, D, CH], F32, name="dc")
-            if DPE[c] == "1":
-                nc.scalar.copy(diff[c][:], banks[c, 1][:])
-                nc.scalar.activation(dd[:], banks[c, 1][:], ACT.Square)
-                nc.scalar.copy(cond[c][:], banks[c, 0][:])
-            else:
-                for ds in parts(c):
-                    nc.scalar.copy(cond[c][:, ds], banks[c, 0][:, ds])
-                for ds in parts(c):
-                    nc.vector.tensor_tensor(diff[c][:, ds], cond[c][:, ds], banks[c, 1][:, ds], ALU.add)
-                for ds in parts(c):
-                    nc.scalar.activation(dd[:, ds], diff[c][:, ds], ACT.Square)
-            nc.scalar.activation(cc[:], banks[c, 0][:], ACT.Square)
-            for ds in parts(c):
-                if DC[c] == "G":
-                    nc.gpsimd.tensor_tensor(dc[:, ds], diff[c][:, ds], cond[c][:, ds], ALU.mult)
-                elif DC[c] == "P":
-                    nc.vector.tensor_tensor(dc[:, ds], diff[c][:, ds], banks[c, 0][:, ds], ALU.mult)
-                else:
-                    nc.vector.tensor_tensor(dc[:, ds], diff[c][:, ds], cond[c][:, ds], ALU.mult)
-            sums[c] = psum.tile([P, 3, V], F32, name="sums", tag="sums")
-            for i, term in enumerate((cc, dd, dc)):
-                for d in range(D):
-                    nc.tensor.matmul(
-                        sums[c][:, i, :], lhsT=term[:, d, :], rhs=ident[:], is_transpose=True, start=(d == 0), stop=(d == D - 1)
-                    )
-
-        hid = keep.tile([P, D, H], BF16, name="hid")
-        spread = {}
-
-        def statistics(c):
-            inv_norm = work.tile([P, V], F32, name="inv_norm")
-            inv_root = work.tile([P, V], F32, name="inv_root")
-            inv_den = work.tile([P, V], F32, name="inv_den")
-            gain = work.tile([P, V], F32, name="gain")
-            num = work.tile([P, V], F32, name="num")
-            shrink = work.tile([P, V], F32, name="shrink")
-            nc.scalar.activation(inv_norm[:], sums[c][:, 1, :], ACT.Abs_reciprocal_sqrt, scale=0.25 / 2.25, bias=0.1 / 2.25)
-            nc.scalar.activation(inv_root[:], sums[c][:, 0, :], ACT.Abs_reciprocal_sqrt, bias=0.3)
-            nc.scalar.activation(gain[:], inv_norm[:], ACT.Copy, scale=unit_sb[:, c : c + 1])
-            nc.scalar.activation(inv_den[:], inv_root[:], ACT.Square)
-            nc.vector.scalar_tensor_tensor(num[:], sums[c][:, 2, :], -1.1 / 1.5, gain[:], ALU.mult, ALU.mult)
-            nc.vector.tensor_tensor(shrink[:], num[:], inv_den[:], ALU.mult)
-            factors = psum.tile([P, 2, CH], F32, name="factors", tag="factors")
-            nc.tensor.transpose(factors[:, 0, :], gain[:], ident[:])
-            for i, term in enumerate((unit_sb[:, c : c + 1].to_broadcast([P, V]), shrink[:])):
-                nc.tensor.matmul(factors[:, 1, :], lhsT=term, rhs=ident[:], is_transpose=True, start=(i == 0), stop=(i == 1))
-            spread[c] = [factors[:, i, :].unsqueeze(1).to_broadcast([P, D, CH]) for i in range(2)]
-
-        def guide(c):
-            along = work.tile([P, D, CH], F32, name="along")
-            across = work.tile([P, D, CH], F32, name="across")
-            for ds in parts(c):
-                nc.vector.tensor_tensor(across[:, ds], diff[c][:, ds], spread[c][0][:, ds], ALU.mult)
-                nc.vector.tensor_tensor(along[:, ds], cond[c][:, ds], spread[c][1][:, ds], ALU.mult)
-            for ds in parts(c):
-                (nc.gpsimd if ADD[c] == "G" else nc.vector).tensor_tensor(
-                    hid[:, ds, CH * c : CH * (c + 1)], along[:, ds], across[:, ds], ALU.add
+        def prepare_weights(side, o):
+            grouped = keep.tile([P, PACK, P, PACK], BF16, name="grouped%d_%d" % (side, o), align_bytes=64)
+            step = P // PACK
+            for q in range(PACK):
+                copy_on(
+                    side == UNCOND or q % 2 == 1,
+                    grouped[:, :, q * step : (q + 1) * step, :].rearrange("p t m j -> p m j t"),
+                    raw[side, o, q].rearrange("p j (m t) -> p m j t", t=PACK),
                 )
+            w_codes[side, o] = keep.tile([P, H], U32, name="w_codes%d_%d" % (side, o), align_bytes=64)
+            w_planes[side, o] = keep.tile([P, H], U8, name="w_planes%d_%d" % (side, o), align_bytes=64)
+            tiles_a_call = 1 if o == PASSES - 1 else PACK
+            for t in range(0, PACK, tiles_a_call):
+                cols = slice(P * t, P * (t + tiles_a_call))
+                values = grouped[:, t : t + tiles_a_call].rearrange("p t m j -> p (t m j)")
+                quantize(w_codes[side, o][:, cols], w_planes[side, o][:, cols], values)
+
+        def rotating_bank(shape, name):
+            return psum.tile(shape, F32, name=name, tag="rotating", bufs=PACK)
+
+        def first_product(side, t):
+            bank = rotating_bank([P, D, GROUPS], "prediction")
+            for o in range(PASSES):
+                nc.tensor.matmul_mx(
+                    out=bank[:].rearrange("p d v -> p (d v)"),
+                    lhsT=w_codes[side, o][:, P * t : P * (t + 1)].bitcast(FP8X4),
+                    lhsT_scale=w_planes[side, o][:, P * t : P * (t + 1)],
+                    rhs=x_codes[o][:].bitcast(FP8X4),
+                    rhs_scale=x_planes[PLANE_ROWS * o : P, :],
+                    start=(o == 0),
+                    stop=(o == PASSES - 1),
+                )
+            return bank
+
+        def add_transposed(dst, terms):
+            for i, term in enumerate(terms):
+                nc.tensor.matmul(dst, lhsT=term, rhs=ident[:], is_transpose=True, start=(i == 0), stop=(i == len(terms) - 1))
+
+        def group_sums(dst, values):
+            add_transposed(dst, [values[:, d, :] for d in range(D)])
+
+        cond = [keep.tile([P, D, GROUPS], F32, name="cond%d" % t) for t in range(PACK)]
+        diff = [keep.tile([P, D, GROUPS], F32, name="diff%d" % t) for t in range(PACK)]
+        inv_den = [keep.tile([P, P], F32, name="inv_den%d" % t) for t in range(PACK)]
+        along = keep.tile([P, PACK, D, GROUPS], F32, name="along")
+        across = keep.tile([P, PACK, D, GROUPS], F32, name="across")
+        uncond, sums, factors = {}, {}, {}
+
+        def denominator(t):
+            cc = work.tile([P, D, GROUPS], F32, name="cc")
+            nc.scalar.activation(cc[:], cond[t][:], ACT.Square)
+            cc_sums = rotating_bank([P, P], "cc_sums")
+            group_sums(cc_sums[:], cc)
+            inv_root = work.tile([P, P], F32, name="inv_root")
+            nc.scalar.activation(inv_root[:], cc_sums[:], ACT.Abs_reciprocal_sqrt, bias=0.3)
+            nc.scalar.activation(inv_den[t][:], inv_root[:], ACT.Square)
+
+        def difference(t):
+            dd = work.tile([P, D, GROUPS], F32, name="dd")
+            dc = work.tile([P, D, GROUPS], F32, name="dc")
+            nc.vector.tensor_tensor(diff[t][:], cond[t][:], uncond[t][:], ALU.subtract)
+            nc.scalar.activation(dd[:], diff[t][:], ACT.Square)
+            nc.vector.tensor_tensor(dc[:], diff[t][:], cond[t][:], ALU.mult)
+            sums[t] = psum.tile([P, 2, P], F32, name="sums", tag="sums")
+            group_sums(sums[t][:, 0, :], dd)
+            group_sums(sums[t][:, 1, :], dc)
+
+        def late_buffer(shape, dtype, name):
+            return work.tile(shape, dtype, name=name, tag="late", bufs=2, align_bytes=64)
+
+        def statistics(t):
+            gain = late_buffer([P, P], F32, "gain")
+            num = work.tile([P, P], F32, name="num")
+            shrink = work.tile([P, P], F32, name="shrink")
+            nc.scalar.activation(
+                gain[:], sums[t][:, 0, :], ACT.Abs_reciprocal_sqrt, scale=1.0 / D / AMPLIFY**2, bias=0.1 / AMPLIFY**2
+            )
+            nc.vector.scalar_tensor_tensor(num[:], sums[t][:, 1, :], -WEAKEN / AMPLIFY, gain[:], ALU.mult, ALU.mult)
+            nc.vector.tensor_tensor(shrink[:], num[:], inv_den[t][:], ALU.mult)
+            factors[t] = psum.tile([P, 2, GROUPS], F32, name="factors", tag="factors")
+            nc.tensor.transpose(factors[t][:, 0, :], gain[:], ident[:])
+            add_transposed(factors[t][:, 1, :], [one[:].to_broadcast([P, P]), shrink[:]])
+
+        def guide(t):
+            for i, (term, values) in enumerate(((across, diff[t]), (along, cond[t]))):
+                factor = factors[t][:, i, :].unsqueeze(1).to_broadcast([P, D, GROUPS])
+                nc.vector.scalar_tensor_tensor(term[:, t], values[:], unit_sb[:, t : t + 1], factor, ALU.mult, ALU.mult)
 
         w3_codes = keep.tile([P, N], U32, name="w3_codes", align_bytes=64)
         w3_planes = keep.tile([P, N], U8, name="w3_planes", align_bytes=64)
 
         def prepare_w3():
-            grouped = keep.tile([P, N, PACK], BF16, name="w3_grouped", align_bytes=64)
-            for half in range(2):
-                cols = slice(half * (N // 2), (half + 1) * (N // 2))
-                interleave(CAST[16 + half], grouped[:, cols, :], w3_raw[:, :, cols], 1.0)
+            grouped = late_buffer([P, N, PACK], BF16, "w3_grouped")
+            nc.scalar.copy(
+                grouped[:].rearrange("p (a i) j -> p a j i", i=LINE), w3_raw[:].rearrange("p j (a i) -> p a j i", i=LINE)
+            )
             quantize(w3_codes[:], w3_planes[:], grouped[:].rearrange("p n j -> p (n j)"))
 
-        gather()
-        prepare_weights(0)
-        products(0)
-        squares(0)
-        prepare_weights(1)
-        products(1)
-        squares(1)
-        prepare_weights(2)
-        products(2)
-        statistics(0)
-        squares(2)
-        prepare_weights(3)
-        products(3)
-        statistics(1)
-        guide(0)
-        squares(3)
-        statistics(2)
-        guide(1)
-        statistics(3)
-        guide(2)
-        guide(3)
+        for side in (COND, UNCOND):
+            for o in range(PASSES):
+                prepare_weights(side, o)
+        for t in range(PACK):
+            nc.scalar.copy(cond[t][:], first_product(COND, t)[:])
+        for t in range(PACK):
+            uncond[t] = first_product(UNCOND, t)
+        for t in range(PACK + 1):
+            if t < PACK:
+                denominator(t)
+                difference(t)
+            if t > 0:
+                statistics(t - 1)
+        for t in range(PACK - 1):
+            guide(t)
         prepare_w3()
+        guide(PACK - 1)
 
-        result = [psum.tile([P, D, V], F32, name="result%d" % h, tag=("sums", "factors")[h]) for h in range(N // P)]
+        result = [psum.tile([P, D, GROUPS], F32, name="result%d" % h, tag="sums") for h in range(N // P)]
         for d in range(D):
-            turned = psum.tile([P, 2, V], F32, name="turned", tag="pred%d" % (d % 2))
-            words = hid[:, d, :].bitcast(F32)
-            for u in range(2):
-                nc.tensor.transpose(turned[:, u, :], words[:, u : H // 2 : 2], ident[:])
-            hid_k = work.tile([P, V, PACK], BF16, name="hid_k", align_bytes=64)
-            copy_out(
-                "SVSV"[d],
-                hid_k[:].rearrange("p v t -> p (v t)").bitcast(F32).rearrange("p (v u) -> p v u", u=2),
-                turned[:].rearrange("p u v -> p v u"),
+            hid = work.tile([P, GROUPS, PACK], BF16, name="hid", align_bytes=64)
+            nc.vector.tensor_tensor(
+                hid[:].rearrange("p (a i) t -> p a t i", i=LINE),
+                along[:, :, d, :].rearrange("p t (a i) -> p a t i", i=LINE),
+                across[:, :, d, :].rearrange("p t (a i) -> p a t i", i=LINE),
+                ALU.add,
             )
-            hid_codes = work.tile([P, V], U32, name="hid_codes", align_bytes=64)
-            hid_planes = work.tile([P, V], U8, name="hid_planes", align_bytes=64)
-            quantize(hid_codes[:], hid_planes[:], hid_k[:].rearrange("p v t -> p (v t)"))
+            hid_codes = work.tile([P, GROUPS], U32, name="hid_codes", align_bytes=64)
+            hid_planes = work.tile([P, GROUPS], U8, name="hid_planes", align_bytes=64)
+            quantize(hid_codes[:], hid_planes[:], hid[:].rearrange("p v t -> p (v t)"))
             for h in range(N // P):
                 nc.tensor.matmul_mx(
                     out=result[h][:, d, :],
@@ -280,11 +242,12 @@ def tile_picked_yapgui_apg_p_kernel(tc, x_words, x_scales, w1, w2, unit, w3, off
                     start=True,
                     stop=True,
                 )
+
         for half in range(2):
             for h in range(N // P):
-                staged = keep.tile([P, V // 2, D], F32, name="staged%d_%d" % (h, half))
-                groups = slice(half * (V // 2), (half + 1) * (V // 2))
-                copy_out("SV"[h], staged[:], result[h][:, :, groups].rearrange("p d v -> p v d"))
+                staged = keep.tile([P, GROUPS // 2, D], F32, name="staged%d_%d" % (h, half))
+                groups = slice(half * (GROUPS // 2), (half + 1) * (GROUPS // 2))
+                copy_on(h == 1, staged[:], result[h][:, :, groups].rearrange("p d v -> p v d"))
                 nc.sync.dma_start(
                     out[P * h : P * (h + 1), half * (S // 2) : (half + 1) * (S // 2)], staged[:].rearrange("p v d -> p (v d)")
                 )

@@ -150,6 +150,7 @@ def tile_picked_yapgui_apg_p_kernel(tc, x_words, x_scales, w1, w2, unit, w3, off
         inv_den = [keep.tile([P, P], F32, name="inv_den%d" % t) for t in range(PACK)]
         along = keep.tile([P, PACK, D, GROUPS], F32, name="along")
         across = keep.tile([P, PACK, D, GROUPS], F32, name="across")
+        hid_tiles = keep.tile([P, PACK, D, GROUPS], BF16, name="hid_tiles")
         uncond, sums, factors = {}, {}, {}
 
         def denominator(t):
@@ -191,6 +192,12 @@ def tile_picked_yapgui_apg_p_kernel(tc, x_words, x_scales, w1, w2, unit, w3, off
             for i, (term, values) in enumerate(((across, diff[t]), (along, cond[t]))):
                 factor = factors[t][:, i, :].unsqueeze(1).to_broadcast([P, D, GROUPS])
                 nc.vector.scalar_tensor_tensor(term[:, t], values[:], unit_sb[:, t : t + 1], factor, ALU.mult, ALU.mult)
+            if t < PACK - 1:
+                nc.gpsimd.tensor_tensor(hid_tiles[:, t], along[:, t], across[:, t], ALU.add)
+            else:
+                for first in range(0, D, 2):
+                    members = slice(first, first + 2)
+                    nc.vector.tensor_tensor(hid_tiles[:, t, members], along[:, t, members], across[:, t, members], ALU.add)
 
         w3_codes = keep.tile([P, N], U32, name="w3_codes", align_bytes=64)
         w3_planes = keep.tile([P, N], U8, name="w3_planes", align_bytes=64)
@@ -223,11 +230,10 @@ def tile_picked_yapgui_apg_p_kernel(tc, x_words, x_scales, w1, w2, unit, w3, off
         result = [psum.tile([P, D, GROUPS], F32, name="result%d" % h, tag="sums") for h in range(N // P)]
         for d in range(D):
             hid = work.tile([P, GROUPS, PACK], BF16, name="hid", align_bytes=64)
-            nc.vector.tensor_tensor(
+            copy_on(
+                d % 2 == 0,
                 hid[:].rearrange("p (a i) t -> p a t i", i=LINE),
-                along[:, :, d, :].rearrange("p t (a i) -> p a t i", i=LINE),
-                across[:, :, d, :].rearrange("p t (a i) -> p a t i", i=LINE),
-                ALU.add,
+                hid_tiles[:, :, d, :].rearrange("p t (a i) -> p a t i", i=LINE),
             )
             hid_codes = work.tile([P, GROUPS], U32, name="hid_codes", align_bytes=64)
             hid_planes = work.tile([P, GROUPS], U8, name="hid_planes", align_bytes=64)

from contextlib import ExitStack

import concourse.mybir as mybir
from concourse.masks import make_identity

K, T, S, D, N, H = 1024, 2048, 512, 4, 256, 512
FLOPS = 2 * (2 * K * H * S + H * N * S)

F32 = mybir.dt.float32
BF16 = mybir.dt.bfloat16
I32 = mybir.dt.int32
U32 = mybir.dt.uint32
U16 = mybir.dt.uint16
U8 = mybir.dt.uint8
FP8X4 = mybir.dt.float8_e4m3fn_x4
ALU = mybir.AluOpType
ACT = mybir.ActivationFunctionType

P = 128
PACK = 4
PASSES = K // (P * PACK)
GROUPS = S // D
PLANE_ROWS = 4
LINE = 4
QUARTER = H // PACK
COND, UNCOND = 0, 1
AMPLIFY = 1.5
WEAKEN = 1.5 - 0.4


def tile_picked_yapgui_apg_p_kernel(tc, x_words, x_scales, w1, w2, unit, w3, offs, out):
    nc = tc.nc
    with ExitStack() as ctx:
        keep = ctx.enter_context(tc.tile_pool(name="keep", bufs=1))
        work = ctx.enter_context(tc.tile_pool(name="work", bufs=PACK))
        psum = ctx.enter_context(tc.psum_pool(name="psum", bufs=2))

        offsets = keep.tile([P, S // 16], U16, name="offsets")
        nc.sync.dma_start(offsets[:], offs)

        scale_table = keep.tile([P, T], U8, name="scale_table", align_bytes=64)
        nc.gpsimd.memset(scale_table[:].bitcast(I32), 0)
        word_table = [keep.tile([P, T], U32, name="word_table%d" % o, align_bytes=64) for o in range(PASSES)]

        def load_words(o, first, last):
            words = x_words[o].rearrange("p n t -> p (n t)").bitcast(I32)
            nc.sync.dma_start(word_table[o][:, first:last].bitcast(I32), words[:, first:last])

        raw = {}

        def load_weights(side, o, pieces):
            span = PACK // pieces
            for first in range(0, PACK, span):
                tile = keep.tile([P, PACK, QUARTER * span], F32, name="raw%d_%d_%d" % (side, o, first))
                rows = (w1, w2)[side][P * PACK * o : P * PACK * (o + 1), QUARTER * first : QUARTER * (first + span)]
                nc.sync.dma_start(tile[:], rows.rearrange("(p j) n -> p j n", j=PACK))
                for q in range(span):
                    raw[side, o, first + q] = tile[:, :, QUARTER * q : QUARTER * (q + 1)]

        load_words(0, 0, T // 2)
        for quadrant in range(P // 32):
            nc.sync.dma_start(
                scale_table[32 * quadrant : 32 * quadrant + PLANE_ROWS * PASSES, :].bitcast(I32),
                x_scales[:, PLANE_ROWS * quadrant : PLANE_ROWS * (quadrant + 1), :].bitcast(I32),
            )
        load_words(0, T // 2, T)
        load_words(1, 0, T)
        load_weights(COND, 0, 1)
        load_weights(COND, 1, 1)
        unit_sb = keep.tile([P, PACK], F32, name="unit_sb")
        nc.sync.dma_start(unit_sb[:], unit.rearrange("(p t) o -> p (t o)", t=PACK))
        load_weights(UNCOND, 0, 1)
        load_weights(UNCOND, 1, 2)
        w3_raw = keep.tile([P, PACK, N], F32, name="w3_raw")
        nc.sync.dma_start(w3_raw[:], w3.rearrange("(p j) n -> p j n", j=PACK))

        warm = keep.tile([P, 2], F32, name="warm")
        nc.vector.memset(warm[:, 0:1], 1.0)
        nc.scalar.activation(warm[:, 1:2], warm[:, 0:1], ACT.Abs_reciprocal_sqrt)

        ident = keep.tile([P, P], F32, name="ident")
        make_identity(nc, ident[:])
        one = keep.tile([P, 1], F32, name="one")
        nc.gpsimd.memset(one[:], 1.0)

        picked_scales = keep.tile([P, S], U8, name="picked_scales", align_bytes=64)
        x_planes = keep.tile([P, S], U8, name="x_planes", align_bytes=64)
        nc.vector.tensor_copy(picked_scales[:], scale_table[:].indirect(offsets[:]))
        nc.vector.tensor_copy(
            x_planes[:].rearrange("p (d v) -> p d v", d=D), picked_scales[:].rearrange("p (v d) -> p d v", d=D)
        )
        x_codes = [keep.tile([P, S], U32, name="x_codes%d" % o, align_bytes=64) for o in range(PASSES)]
        for o in range(PASSES):
            nc.vector.tensor_copy(x_codes[o][:].rearrange("p (d v) -> p v d", d=D), word_table[o][:].indirect(offsets[:]))

        def copy_on(vector, dst, src):
            if vector:
                nc.vector.tensor_copy(dst, src)
            else:
                nc.scalar.copy(dst, src)

        def quantize(codes, planes, values):
            nc.vector.quantize_mx(out=codes.bitcast(FP8X4), scales=planes, in_=values)

        w_codes, w_planes = {}, {}

        def prepare_weights(side, o):
            grouped = keep.tile([P, PACK, P, PACK], BF16, name="grouped%d_%d" % (side, o), align_bytes=64)
            step = P // PACK
            for q in range(PACK):
                copy_on(
                    side == UNCOND or q % 2 == 1,
                    grouped[:, :, q * step : (q + 1) * step, :].rearrange("p t m j -> p m j t"),
                    raw[side, o, q].rearrange("p j (m t) -> p m j t", t=PACK),
                )
            w_codes[side, o] = keep.tile([P, H], U32, name="w_codes%d_%d" % (side, o), align_bytes=64)
            w_planes[side, o] = keep.tile([P, H], U8, name="w_planes%d_%d" % (side, o), align_bytes=64)
            tiles_a_call = 1 if o == PASSES - 1 else PACK
            for t in range(0, PACK, tiles_a_call):
                cols = slice(P * t, P * (t + tiles_a_call))
                values = grouped[:, t : t + tiles_a_call].rearrange("p t m j -> p (t m j)")
                quantize(w_codes[side, o][:, cols], w_planes[side, o][:, cols], values)

        def rotating_bank(shape, name):
            return psum.tile(shape, F32, name=name, tag="rotating", bufs=PACK)

        def first_product(side, t):
            bank = rotating_bank([P, D, GROUPS], "prediction")
            for o in range(PASSES):
                nc.tensor.matmul_mx(
                    out=bank[:].rearrange("p d v -> p (d v)"),
                    lhsT=w_codes[side, o][:, P * t : P * (t + 1)].bitcast(FP8X4),
                    lhsT_scale=w_planes[side, o][:, P * t : P * (t + 1)],
                    rhs=x_codes[o][:].bitcast(FP8X4),
                    rhs_scale=x_planes[PLANE_ROWS * o : P, :],
                    start=(o == 0),
                    stop=(o == PASSES - 1),
                )
            return bank

        def add_transposed(dst, terms):
            for i, term in enumerate(terms):
                nc.tensor.matmul(dst, lhsT=term, rhs=ident[:], is_transpose=True, start=(i == 0), stop=(i == len(terms) - 1))

        def group_sums(dst, values):
            add_transposed(dst, [values[:, d, :] for d in range(D)])

        cond = [keep.tile([P, D, GROUPS], F32, name="cond%d" % t) for t in range(PACK)]
        diff = [keep.tile([P, D, GROUPS], F32, name="diff%d" % t) for t in range(PACK)]
        inv_den = [keep.tile([P, P], F32, name="inv_den%d" % t) for t in range(PACK)]
        along = keep.tile([P, PACK, D, GROUPS], F32, name="along")
        across = keep.tile([P, PACK, D, GROUPS], F32, name="across")
        hid_tiles = keep.tile([P, PACK, D, GROUPS], BF16, name="hid_tiles")
        uncond, sums, factors = {}, {}, {}

        def denominator(t):
            cc = work.tile([P, D, GROUPS], F32, name="cc")
            nc.scalar.activation(cc[:], cond[t][:], ACT.Square)
            cc_sums = rotating_bank([P, P], "cc_sums")
            group_sums(cc_sums[:], cc)
            inv_root = work.tile([P, P], F32, name="inv_root")
            nc.scalar.activation(inv_root[:], cc_sums[:], ACT.Abs_reciprocal_sqrt, bias=0.3)
            nc.scalar.activation(inv_den[t][:], inv_root[:], ACT.Square)

        def difference(t):
            dd = work.tile([P, D, GROUPS], F32, name="dd")
            dc = work.tile([P, D, GROUPS], F32, name="dc")
            nc.vector.tensor_tensor(diff[t][:], cond[t][:], uncond[t][:], ALU.subtract)
            nc.scalar.activation(dd[:], diff[t][:], ACT.Square)
            nc.vector.tensor_tensor(dc[:], diff[t][:], cond[t][:], ALU.mult)
            sums[t] = psum.tile([P, 2, P], F32, name="sums", tag="sums")
            group_sums(sums[t][:, 0, :], dd)
            group_sums(sums[t][:, 1, :], dc)

        def late_buffer(shape, dtype, name):
            return work.tile(shape, dtype, name=name, tag="late", bufs=2, align_bytes=64)

        def statistics(t):
            gain = late_buffer([P, P], F32, "gain")
            num = work.tile([P, P], F32, name="num")
            shrink = work.tile([P, P], F32, name="shrink")
            nc.scalar.activation(
                gain[:], sums[t][:, 0, :], ACT.Abs_reciprocal_sqrt, scale=1.0 / D / AMPLIFY**2, bias=0.1 / AMPLIFY**2
            )
            nc.vector.scalar_tensor_tensor(num[:], sums[t][:, 1, :], -WEAKEN / AMPLIFY, gain[:], ALU.mult, ALU.mult)
            nc.vector.tensor_tensor(shrink[:], num[:], inv_den[t][:], ALU.mult)
            factors[t] = psum.tile([P, 2, GROUPS], F32, name="factors", tag="factors")
            nc.tensor.transpose(factors[t][:, 0, :], gain[:], ident[:])
            add_transposed(factors[t][:, 1, :], [one[:].to_broadcast([P, P]), shrink[:]])

        def guide(t):
            for i, (term, values) in enumerate(((across, diff[t]), (along, cond[t]))):
                factor = factors[t][:, i, :].unsqueeze(1).to_broadcast([P, D, GROUPS])
                nc.vector.scalar_tensor_tensor(term[:, t], values[:], unit_sb[:, t : t + 1], factor, ALU.mult, ALU.mult)
            if t < PACK - 1:
                nc.gpsimd.tensor_tensor(hid_tiles[:, t], along[:, t], across[:, t], ALU.add)
            else:
                for first in range(0, D, 2):
                    members = slice(first, first + 2)
                    nc.vector.tensor_tensor(hid_tiles[:, t, members], along[:, t, members], across[:, t, members], ALU.add)

        w3_codes = keep.tile([P, N], U32, name="w3_codes", align_bytes=64)
        w3_planes = keep.tile([P, N], U8, name="w3_planes", align_bytes=64)

        def prepare_w3():
            grouped = late_buffer([P, N, PACK], BF16, "w3_grouped")
            nc.scalar.copy(
                grouped[:].rearrange("p (a i) j -> p a j i", i=LINE), w3_raw[:].rearrange("p j (a i) -> p a j i", i=LINE)
            )
            quantize(w3_codes[:], w3_planes[:], grouped[:].rearrange("p n j -> p (n j)"))

        for side in (COND, UNCOND):
            for o in range(PASSES):
                prepare_weights(side, o)
        for t in range(PACK):
            nc.scalar.copy(cond[t][:], first_product(COND, t)[:])
        for t in range(PACK):
            uncond[t] = first_product(UNCOND, t)
        for t in range(PACK + 1):
            if t < PACK:
                denominator(t)
                difference(t)
            if t > 0:
                statistics(t - 1)
        for t in range(PACK - 1):
            guide(t)
        prepare_w3()
        guide(PACK - 1)

        result = [psum.tile([P, D, GROUPS], F32, name="result%d" % h, tag="sums") for h in range(N // P)]
        for d in range(D):
            hid = work.tile([P, GROUPS, PACK], BF16, name="hid", align_bytes=64)
            copy_on(
                d % 2 == 0,
                hid[:].rearrange("p (a i) t -> p a t i", i=LINE),
                hid_tiles[:, :, d, :].rearrange("p t (a i) -> p a t i", i=LINE),
            )
            hid_codes = work.tile([P, GROUPS], U32, name="hid_codes", align_bytes=64)
            hid_planes = work.tile([P, GROUPS], U8, name="hid_planes", align_bytes=64)
            quantize(hid_codes[:], hid_planes[:], hid[:].rearrange("p v t -> p (v t)"))
            for h in range(N // P):
                nc.tensor.matmul_mx(
                    out=result[h][:, d, :],
                    lhsT=w3_codes[:, P * h : P * (h + 1)].bitcast(FP8X4),
                    lhsT_scale=w3_planes[:, P * h : P * (h + 1)],
                    rhs=hid_codes[:].bitcast(FP8X4),
                    rhs_scale=hid_planes[:],
                    start=True,
                    stop=True,
                )

        for half in range(2):
            for h in range(N // P):
                staged = keep.tile([P, GROUPS // 2, D], F32, name="staged%d_%d" % (h, half))
                groups = slice(half * (GROUPS // 2), (half + 1) * (GROUPS // 2))
                copy_on(h == 1, staged[:], result[h][:, :, groups].rearrange("p d v -> p v d"))
                nc.sync.dma_start(
                    out[P * h : P * (h + 1), half * (S // 2) : (half + 1) * (S // 2)], staged[:].rearrange("p v d -> p (v d)")
                )
